import numpy as np
import ml_dtypes


def mxq(x, axis, fmt="e4m3"):
    dtype, down = {"e4m3": (ml_dtypes.float8_e4m3fn, 7), "e5m2": (ml_dtypes.float8_e5m2, 14)}[fmt]
    v = np.moveaxis(np.asarray(x, np.float32).astype(ml_dtypes.bfloat16).astype(np.float64), axis, -1)
    blocks = v.reshape(v.shape[:-1] + (-1, 32))
    amax = np.abs(blocks).max(-1, keepdims=True)
    byte = np.maximum(np.where(amax > 0, np.frexp(amax)[1] - 1 + 127, 0) - down, 1)
    scale = np.exp2(byte - 127.0)
    codes = (blocks / scale).astype(np.float32).astype(dtype).astype(np.float64)
    return np.moveaxis((codes * scale).reshape(v.shape), -1, axis)


WIDE = False


def mx_kscale(k):
    if not WIDE:
        return np.ones(k)
    levels = np.array([30, -30])
    if k % 512:
        return np.exp2(np.random.permutation(np.resize(levels, k // 32))).repeat(32)
    a = np.empty((k // 512, 16))
    for p in range(k // 512):
        a[p, :8] = np.random.permutation(np.resize(levels, 8))
        for g in range(8):
            far = levels[np.abs(levels - a[p, g]) >= 10]
            a[p, g + 8] = far[np.random.randint(len(far))]
    return np.exp2(a.ravel()).repeat(32)


def f64(x):
    return np.asarray(x).astype(np.float64)


def striped(idx):
    return np.tile(idx.reshape(-1, 16).T, (8, 1)).astype(np.uint16)


def unstriped(offs):
    return offs[:16].T.reshape(-1).astype(np.int64)


E2M1 = np.array([0.0, 0.5, 1.0, 1.5, 2.0, 3.0, 4.0, 6.0, -0.0, -0.5, -1.0, -1.5, -2.0, -3.0, -4.0, -6.0])


def pack_weight(w, fmt):
    k, n = w.shape
    w = f64(np.asarray(w, np.float32).astype(ml_dtypes.bfloat16)).reshape(k // 32, 32, n)
    amax = np.abs(w).max(1)
    if fmt == "e4m3":
        byte = np.frexp(amax)[1] - 1 + 127 - 7
    elif fmt == "e5m2":
        byte = np.frexp(amax)[1] - 1 + 127 - 14
    else:
        mant, ex = np.frexp(amax / 6.0)
        byte = np.where(mant > 0.5, ex, ex - 1) + 127
    byte = np.clip(np.where(amax > 0, byte, 1), 1, 254)
    scaled = (w * np.exp2(127.0 - byte)[:, None, :]).reshape(k, n).astype(np.float32)
    by_word = np.ascontiguousarray(scaled.reshape(k // 512, 128, 4, n).transpose(0, 1, 3, 2))
    if fmt == "e4m3":
        words = by_word.astype(ml_dtypes.float8_e4m3fn).view(np.uint8)
    elif fmt == "e5m2":
        words = by_word.astype(ml_dtypes.float8_e5m2).view(np.uint8)
    else:
        c = by_word.astype(ml_dtypes.float4_e2m1fn).view(np.uint8) & 0xF
        words = (c[..., 0::2] | (c[..., 1::2] << 4)).reshape(k // 512, 128, 2 * n)
    return np.ascontiguousarray(words), np.ascontiguousarray(byte.astype(np.uint8).reshape(k // 512, 16, n))


def unpack_weight(words, scales, fmt):
    g, _, n = scales.shape
    words = np.ascontiguousarray(words).reshape(g, 128, n, -1)
    if fmt == "e4m3":
        vals = words.view(ml_dtypes.float8_e4m3fn).astype(np.float64)
    elif fmt == "e5m2":
        vals = words.view(ml_dtypes.float8_e5m2).astype(np.float64)
    else:
        nib = np.empty((g, 128, n, 4), np.uint8)
        nib[..., 0::2] = words & 0xF
        nib[..., 1::2] = words >> 4
        vals = E2M1[nib]
    vals = vals * np.repeat(np.exp2(scales.astype(np.float64) - 127.0), 8, axis=1)[..., None]
    return vals.transpose(0, 1, 3, 2).reshape(g * 512, n)


def relu(v):
    return np.maximum(v, 0.0)


def d_relu(v):
    return (v > 0).astype(np.float64)


K, T, E, C, H, N = 256, 1024, 4, 512, 512, 1024


def by_expert(wq, xq):
    return np.concatenate([wq[e].T @ xq[:, e * C:(e + 1) * C] for e in range(E)], axis=1)


def setup_inputs():
    n = np.random.standard_normal
    s = mx_kscale(N)[:, None]
    u = mx_kscale(H)
    first = np.random.permutation(np.repeat(np.arange(E), T // E))
    second = (first + 1 + np.random.permutation(np.repeat(np.arange(E - 1), -(-T // (E - 1)))[:T])) % E
    while np.bincount(second, minlength=E).max() != T // E:
        load = np.bincount(second, minlength=E); hi, lo = int(load.argmax()), int(load.argmin())
        t = np.flatnonzero((second == hi) & (first != lo))[0]; second[t] = lo
    slot_token = np.empty(E * C, np.int64); pos = np.empty((2, T), np.int64); fill = np.zeros(E, np.int64)
    place = np.stack([np.random.permutation(C) for _ in range(E)])
    for r, deal in enumerate((first, second)):
        for t in np.random.permutation(T):
            e = deal[t]; j = e * C + place[e, fill[e]]; fill[e] += 1; slot_token[j] = t; pos[r, t] = j
    g = np.random.uniform(0.2, 0.8, T)
    w_slot = np.empty(E * C); w_slot[pos[0]] = g; w_slot[pos[1]] = 1.0 - g
    dy = pack_weight(n((N, T)) * s, "e5m2")
    w2 = [pack_weight(m, "e2m1") for m in n((E, N, H)) / np.sqrt(N) / s[None] * u[None, None, :]]
    w1 = [pack_weight(m, "e2m1") for m in n((E, H, K)) / np.sqrt(H) / u[None, :, None]]
    w3 = [pack_weight(m, "e2m1") for m in n((E, H, K)) / np.sqrt(H) / u[None, :, None]]
    return {
        "dy_words": dy[0],
        "dy_scales": dy[1],
        "a1": n((H, E * C)).astype(np.float32),
        "a3": n((H, E * C)).astype(np.float32),
        "w2_words": np.stack([m[0] for m in w2]),
        "w2_scales": np.stack([m[1] for m in w2]),
        "w1_words": np.stack([m[0] for m in w1]),
        "w1_scales": np.stack([m[1] for m in w1]),
        "w3_words": np.stack([m[0] for m in w3]),
        "w3_scales": np.stack([m[1] for m in w3]),
        "gate": np.tile(w_slot, (H, 1)).astype(np.float32),
        "offs": striped(slot_token),
        "pos1": striped(pos[0]),
        "pos2": striped(pos[1]),
    }


def reference(dy_words, dy_scales, a1, a3, w2_words, w2_scales, w1_words, w1_scales, w3_words, w3_scales, gate, offs, pos1, pos2):
    idx = unstriped(offs)
    w2 = np.stack([unpack_weight(w2_words[e], w2_scales[e], "e2m1") for e in range(E)])
    w1 = np.stack([unpack_weight(w1_words[e], w1_scales[e], "e2m1") for e in range(E)])
    w3 = np.stack([unpack_weight(w3_words[e], w3_scales[e], "e2m1") for e in range(E)])
    gq = unpack_weight(dy_words, dy_scales, "e5m2")[:, idx]
    dh = f64(gate) * by_expert(w2, gq)
    da1 = dh * f64(a3) * d_relu(f64(a1))
    da3 = dh * relu(f64(a1))
    dx = by_expert(w1, mxq(da1, 0, "e5m2")) + by_expert(w3, mxq(da3, 0, "e5m2"))
    return dx[:, unstriped(pos1)] + dx[:, unstriped(pos2)]

@@ -1,0 +1,222 @@
+from contextlib import ExitStack
+
+import concourse.mybir as mybir
+from concourse.masks import make_identity
+
+K, T, E, C, H, N = 256, 1024, 4, 512, 512, 1024
+S = E * C
+FLOPS = 2 * S * (N * H + 2 * H * K)
+
+F32 = mybir.dt.float32
+BF16 = mybir.dt.bfloat16
+I32 = mybir.dt.int32
+U32 = mybir.dt.uint32
+U16 = mybir.dt.uint16
+U8 = mybir.dt.uint8
+E5M2 = mybir.dt.float8_e5m2_x4
+E2M1 = mybir.dt.float4_e2m1fn_x4
+ACT = mybir.ActivationFunctionType
+MULT = mybir.AluOpType.mult
+ADD = mybir.AluOpType.add
+
+P = 128
+PACK = 4
+PASSES = N // (P * PACK)
+BLOCKS = C // P
+KB = K // P
+LIST_COLS = C // 16
+SHIFT = 16
+
+
+def tile_moe_bdx_glu_relu_kernel(
+    tc, dy_words, dy_scales, a1, a3, w2_words, w2_scales, w1_words, w1_scales, w3_words, w3_scales,
+    gate, offs, pos1, pos2, out,
+):
+    nc = tc.nc
+    with ExitStack() as ctx:
+        lists = ctx.enter_context(tc.tile_pool(name="lists", bufs=1))
+        keep = ctx.enter_context(tc.tile_pool(name="keep", bufs=1))
+        ring = ctx.enter_context(tc.tile_pool(name="ring", bufs=2))
+        psum = ctx.enter_context(tc.psum_pool(name="psum", bufs=1))
+
+        offs_sb = lists.tile([P, S // 16], U16, name="offs_sb")
+        pos1_sb = lists.tile([P, T // 16], U16, name="pos1_sb")
+        pos2_sb = lists.tile([P, T // 16], U16, name="pos2_sb")
+
+        dy_plane = keep.tile([P, T], U8, name="dy_plane", align_bytes=64)
+        w2_plane = keep.tile([P, E * PASSES * H], U8, name="w2_plane", align_bytes=64)
+        w1_plane = keep.tile([P, E * K], U8, name="w1_plane", align_bytes=64)
+        w3_plane = keep.tile([P, E * K], U8, name="w3_plane", align_bytes=64)
+        g_plane0 = keep.tile([P, S], U8, name="g_plane0", align_bytes=64)
+        g_plane1 = keep.tile([P, S], U8, name="g_plane1", align_bytes=64)
+        for plane in (dy_plane, w2_plane, g_plane1, w1_plane, w3_plane):
+            nc.vector.memset(plane[:].bitcast(I32), 0)
+        gate_rows = keep.tile([P, P], F32, name="gate_rows")
+        nc.gpsimd.memset(gate_rows[:], 0.0)
+        ident = keep.tile([P, P], F32, name="ident")
+        make_identity(nc, ident[:])
+
+        def load_act(src, name, e):
+            t = keep.tile([P, PACK, C], F32, name=f"{name}{e}")
+            nc.sync.dma_start(out=t[:], in_=src[:, e * C:(e + 1) * C].rearrange("(p t) c -> p t c", t=PACK))
+            return t
+
+        def load_plane(plane, scales, width):
+            for r in range(4):
+                nc.sync.dma_start(
+                    out=plane[r:P:32, :].bitcast(I32).rearrange("q (g c) -> q g c", c=width // 4),
+                    in_=scales[:, :, r:16:4, :].rearrange("e s q c -> q (e s) c").bitcast(I32),
+                )
+
+        def load_words(words, name):
+            groups, width = words.shape[0] * words.shape[1], words.shape[3]
+            t = keep.tile([P, groups * width], U8, name=name, align_bytes=64)
+            nc.sync.dma_start(
+                out=t[:].bitcast(I32).rearrange("p (g c) -> p g c", g=groups),
+                in_=words.rearrange("e s p c -> p (e s) c").bitcast(I32),
+            )
+            return t
+
+        nc.sync.dma_start(offs_sb[:], offs)
+        for r in range(4):
+            nc.sync.dma_start(
+                out=dy_plane[r:P:SHIFT, :].bitcast(I32),
+                in_=dy_scales[:, r:16:4, :].rearrange("o q c -> q o c").bitcast(I32),
+            )
+        dy_sb = []
+        for o in range(PASSES):
+            t = keep.tile([P, T], U32, name=f"dy{o}", align_bytes=64)
+            nc.sync.dma_start(out=t[:].bitcast(I32), in_=dy_words[o].rearrange("p t d -> p (t d)").bitcast(I32))
+            dy_sb.append(t)
+        a1_sb, a3_sb = [None] * E, [None] * E
+        a1_sb[0] = load_act(a1, "a1_", 0)
+        nc.sync.dma_start(out=gate_rows[0:S // P, :], in_=gate[0:1, :].rearrange("o (b c) -> (o b) c", c=P))
+        load_plane(w2_plane, w2_scales, H)
+        w2_sb = load_words(w2_words, "w2_sb")
+        a1_sb[1] = load_act(a1, "a1_", 1)
+        a3_sb[0] = load_act(a3, "a3_", 0)
+        a1_sb[2] = load_act(a1, "a1_", 2)
+        load_plane(w1_plane, w1_scales, K)
+        load_plane(w3_plane, w3_scales, K)
+        w1_sb = load_words(w1_words, "w1_sb")
+        w3_sb = load_words(w3_words, "w3_sb")
+        a3_sb[1] = load_act(a3, "a3_", 1)
+        a1_sb[3] = load_act(a1, "a1_", 3)
+        a3_sb[2] = load_act(a3, "a3_", 2)
+        a3_sb[3] = load_act(a3, "a3_", 3)
+        nc.sync.dma_start(pos1_sb[:], pos1)
+        nc.sync.dma_start(pos2_sb[:], pos2)
+
+        gate_ps = psum.tile([P, C], F32, name="gate_ps", tag="x", bufs=2)
+        nc.tensor.transpose(gate_ps[:, 0:P], gate_rows[:], ident[:])
+        gate_col = keep.tile([P, S // P], F32, name="gate_col")
+        nc.scalar.copy(out=gate_col[:], in_=gate_ps[:, 0:S // P])
+
+        def slots_of(e):
+            return offs_sb[:, e * LIST_COLS:(e + 1) * LIST_COLS]
+
+        for e in range(E):
+            nc.vector.tensor_copy(out=g_plane0[:, e * C:(e + 1) * C], in_=dy_plane[:].indirect(slots_of(e)))
+        nc.scalar.dma_start(out=g_plane1[0:P - SHIFT, :].bitcast(I32), in_=g_plane0[SHIFT:P, :].bitcast(I32))
+        g_planes = (g_plane0, g_plane1)
+        g_words = {}
+        for e in range(E):
+            for o in range(PASSES):
+                t = keep.tile([P, C], U32, name=f"g{e}_{o}", align_bytes=64)
+                nc.vector.tensor_copy(out=t[:], in_=dy_sb[o][:].indirect(slots_of(e)))
+                g_words[e, o] = t
+
+        dx = [keep.tile([P, S], F32, name=f"dx{kb}") for kb in range(KB)]
+
+        def by_pairs(rows):
+            return rows.rearrange("p t (c i) -> p c t i", i=2)
+
+        def packed_by_pairs(cols):
+            return cols.rearrange("p (c i) t -> p c t i", i=2)
+
+        def first_product(e):
+            turned = []
+            for j in range(BLOCKS):
+                b = e * BLOCKS + j
+                acc = psum.tile([P, H], F32, name="acc", tag="h", bufs=2)
+                for o in range(PASSES):
+                    g = e * PASSES + o
+                    nc.tensor.matmul_mx(
+                        out=acc[:],
+                        lhsT=g_words[e, o][:, j * P:(j + 1) * P].bitcast(E5M2),
+                        lhsT_scale=g_planes[o][:, b * P:(b + 1) * P],
+                        rhs=w2_sb[:, g * 2 * H:(g + 1) * 2 * H].bitcast(E2M1),
+                        rhs_scale=w2_plane[:, g * H:(g + 1) * H],
+                        start=(o == 0),
+                        stop=(o == PASSES - 1),
+                    )
+                dh_t = keep.tile([P, PACK, P], F32, name=f"dh_t{b}")
+                nc.scalar.activation(
+                    out=dh_t[:], in_=acc[:].rearrange("p (m t) -> p t m", t=PACK), func=ACT.Copy,
+                    scale=gate_col[:, b:b + 1],
+                )
+                turned.append(dh_t)
+            return turned
+
+        def masks_of(e):
+            relu = a1_sb[e]
+            nc.scalar.activation(out=relu[:], in_=a1_sb[e][:], func=ACT.Relu)
+            step = keep.tile([P, C, PACK], BF16, name=f"step{e}")
+            nc.scalar.activation(out=packed_by_pairs(step[:]), in_=by_pairs(relu[:]), func=ACT.Sign)
+            return relu, step
+
+        def quantise(da, name):
+            codes = ring.tile([P, C], U32, name=f"{name}_codes", align_bytes=64)
+            plane = ring.tile([P, C], U8, name=f"{name}_plane", align_bytes=64)
+            nc.vector.quantize_mx(out=codes[:].bitcast(E5M2), scales=plane[:], in_=da[:].rearrange("p c t -> p (c t)"))
+            return codes, plane
+
+        def second_product(e, turned, relu, step):
+            da1_full = ring.tile([P, C, PACK], BF16, name="da1_full", align_bytes=64)
+            da1 = ring.tile([P, C, PACK], BF16, name="da1", align_bytes=64)
+            da3 = ring.tile([P, C, PACK], BF16, name="da3", align_bytes=64)
+            for j in range(BLOCKS):
+                cols = slice(j * P, (j + 1) * P)
+                dh = psum.tile([P, PACK, P], F32, name="dh", tag="d", bufs=4)
+                for t in range(PACK):
+                    nc.tensor.transpose(dh[:, t, :], turned[j][:, t, :], ident[:])
+                nc.vector.tensor_tensor(
+                    out=packed_by_pairs(da1_full[:, cols, :]), in0=by_pairs(dh[:]), in1=by_pairs(a3_sb[e][:, :, cols]), op=MULT)
+                nc.vector.tensor_tensor(
+                    out=packed_by_pairs(da3[:, cols, :]), in0=by_pairs(dh[:]), in1=by_pairs(relu[:, :, cols]), op=MULT)
+            nc.vector.tensor_tensor(out=da1[:], in0=da1_full[:], in1=step[:], op=MULT)
+            q3 = quantise(da3, "da3")
+            q1 = quantise(da1, "da1")
+            for kb in range(KB):
+                acc = psum.tile([P, C], F32, name="dx_ps", tag="x", bufs=2)
+                for i, (w_sb, w_plane, (codes, plane)) in enumerate(((w3_sb, w3_plane, q3), (w1_sb, w1_plane, q1))):
+                    c0 = e * K + kb * P
+                    nc.tensor.matmul_mx(
+                        out=acc[:],
+                        lhsT=w_sb[:, 2 * c0:2 * (c0 + P)].bitcast(E2M1),
+                        lhsT_scale=w_plane[:, c0:c0 + P],
+                        rhs=codes[:].bitcast(E5M2),
+                        rhs_scale=plane[:],
+                        start=(i == 0),
+                        stop=(i == 1),
+                    )
+                nc.scalar.copy(out=dx[kb][:, e * C:(e + 1) * C], in_=acc[:])
+
+        ready = []
+        for e in range(E):
+            turned = first_product(e)
+            ready.append((turned,) + masks_of(e))
+        for e in range(E):
+            second_product(e, *ready[e])
+
+        firsts = []
+        for kb in range(KB):
+            first = keep.tile([P, T], F32, name=f"first{kb}")
+            nc.vector.tensor_copy(out=first[:], in_=dx[kb][:].indirect(pos1_sb[:]))
+            firsts.append(first)
+        pieces = [(0, 0, T), (1, 0, T // 2), (1, T // 2, T // 4), (1, 3 * T // 4, T // 4)]
+        for kb, t0, n in pieces:
+            both = keep.tile([P, n], F32, name=f"both{kb}_{t0}")
+            nc.vector.tensor_tensor(
+                out=both[:], in0=dx[kb][:].indirect(pos2_sb[:, t0 // 16:(t0 + n) // 16]), in1=firsts[kb][:, t0:t0 + n], op=ADD)
+            nc.sync.dma_start(out=out[kb * P:(kb + 1) * P, t0:t0 + n], in_=both[:])

@@ -49,7 +49,8 @@ def tile_moe_bdx_glu_relu_kernel(
         w3_plane = keep.tile([P, E * K], U8, name="w3_plane", align_bytes=64)
         g_plane0 = keep.tile([P, S], U8, name="g_plane0", align_bytes=64)
         g_plane1 = keep.tile([P, S], U8, name="g_plane1", align_bytes=64)
-        for plane in (dy_plane, w2_plane, g_plane1, w1_plane, w3_plane):
+        nc.gpsimd.memset(dy_plane[:].bitcast(I32), 0)
+        for plane in (w2_plane, g_plane1, w1_plane, w3_plane):
             nc.vector.memset(plane[:].bitcast(I32), 0)
         gate_rows = keep.tile([P, P], F32, name="gate_rows")
         nc.gpsimd.memset(gate_rows[:], 0.0)
@@ -83,16 +84,23 @@ def tile_moe_bdx_glu_relu_kernel(
                 out=dy_plane[r:P:SHIFT, :].bitcast(I32),
                 in_=dy_scales[:, r:16:4, :].rearrange("o q c -> q o c").bitcast(I32),
             )
+        a1_sb, a3_sb = [None] * E, [None] * E
+        a1_sb[0] = load_act(a1, "a1_", 0)
         dy_sb = []
         for o in range(PASSES):
             t = keep.tile([P, T], U32, name=f"dy{o}", align_bytes=64)
             nc.sync.dma_start(out=t[:].bitcast(I32), in_=dy_words[o].rearrange("p t d -> p (t d)").bitcast(I32))
             dy_sb.append(t)
-        a1_sb, a3_sb = [None] * E, [None] * E
-        a1_sb[0] = load_act(a1, "a1_", 0)
         nc.sync.dma_start(out=gate_rows[0:S // P, :], in_=gate[0:1, :].rearrange("o (b c) -> (o b) c", c=P))
         load_plane(w2_plane, w2_scales, H)
         w2_sb = load_words(w2_words, "w2_sb")
+
+        def slots_of(e):
+            return offs_sb[:, e * LIST_COLS:(e + 1) * LIST_COLS]
+
+        for e in range(E):
+            nc.vector.tensor_copy(out=g_plane0[:, e * C:(e + 1) * C], in_=dy_plane[:].indirect(slots_of(e)))
+        nc.sync.dma_start(out=g_plane1[0:P - SHIFT, :].bitcast(I32), in_=g_plane0[SHIFT:P, :].bitcast(I32))
         a1_sb[1] = load_act(a1, "a1_", 1)
         a3_sb[0] = load_act(a3, "a3_", 0)
         a1_sb[2] = load_act(a1, "a1_", 2)
@@ -112,12 +120,6 @@ def tile_moe_bdx_glu_relu_kernel(
         gate_col = keep.tile([P, S // P], F32, name="gate_col")
         nc.scalar.copy(out=gate_col[:], in_=gate_ps[:, 0:S // P])
 
-        def slots_of(e):
-            return offs_sb[:, e * LIST_COLS:(e + 1) * LIST_COLS]
-
-        for e in range(E):
-            nc.vector.tensor_copy(out=g_plane0[:, e * C:(e + 1) * C], in_=dy_plane[:].indirect(slots_of(e)))
-        nc.scalar.dma_start(out=g_plane1[0:P - SHIFT, :].bitcast(I32), in_=g_plane0[SHIFT:P, :].bitcast(I32))
         g_planes = (g_plane0, g_plane1)
         g_words = {}
         for e in range(E):

@@ -57,9 +57,11 @@ def tile_moe_bdx_glu_relu_kernel(
         ident = keep.tile([P, P], F32, name="ident")
         make_identity(nc, ident[:])
 
-        def load_act(src, name, e):
+        def load_act(src, name, e, parts=1):
             t = keep.tile([P, PACK, C], F32, name=f"{name}{e}")
-            nc.sync.dma_start(out=t[:], in_=src[:, e * C:(e + 1) * C].rearrange("(p t) c -> p t c", t=PACK))
+            for c0 in range(0, C, C // parts):
+                c1 = c0 + C // parts
+                nc.sync.dma_start(out=t[:, :, c0:c1], in_=src[:, e * C + c0:e * C + c1].rearrange("(p t) c -> p t c", t=PACK))
             return t
 
         def load_plane(plane, scales, width):
@@ -84,16 +86,19 @@ def tile_moe_bdx_glu_relu_kernel(
                 out=dy_plane[r:P:SHIFT, :].bitcast(I32),
                 in_=dy_scales[:, r:16:4, :].rearrange("o q c -> q o c").bitcast(I32),
             )
-        a1_sb, a3_sb = [None] * E, [None] * E
-        a1_sb[0] = load_act(a1, "a1_", 0)
-        dy_sb = []
-        for o in range(PASSES):
+        def load_dy(o):
             t = keep.tile([P, T], U32, name=f"dy{o}", align_bytes=64)
             nc.sync.dma_start(out=t[:].bitcast(I32), in_=dy_words[o].rearrange("p t d -> p (t d)").bitcast(I32))
-            dy_sb.append(t)
+            return t
+
+        a1_sb, a3_sb = [None] * E, [None] * E
+        a1_sb[0] = load_act(a1, "a1_", 0, parts=2)
+        dy_sb = [load_dy(0)]
+        a1_sb[1] = load_act(a1, "a1_", 1)
+        dy_sb.append(load_dy(1))
         nc.sync.dma_start(out=gate_rows[0:S // P, :], in_=gate[0:1, :].rearrange("o (b c) -> (o b) c", c=P))
         load_plane(w2_plane, w2_scales, H)
-        w2_sb = load_words(w2_words, "w2_sb")
+        w2_sb = [load_words(w2_words[0:E // 2], "w2_lo")]
 
         def slots_of(e):
             return offs_sb[:, e * LIST_COLS:(e + 1) * LIST_COLS]
@@ -101,7 +106,7 @@ def tile_moe_bdx_glu_relu_kernel(
         for e in range(E):
             nc.vector.tensor_copy(out=g_plane0[:, e * C:(e + 1) * C], in_=dy_plane[:].indirect(slots_of(e)))
         nc.sync.dma_start(out=g_plane1[0:P - SHIFT, :].bitcast(I32), in_=g_plane0[SHIFT:P, :].bitcast(I32))
-        a1_sb[1] = load_act(a1, "a1_", 1)
+        w2_sb.append(load_words(w2_words[E // 2:E], "w2_hi"))
         a3_sb[0] = load_act(a3, "a3_", 0)
         a1_sb[2] = load_act(a1, "a1_", 2)
         load_plane(w1_plane, w1_scales, K)
@@ -147,12 +152,12 @@ def tile_moe_bdx_glu_relu_kernel(
                         out=acc[:],
                         lhsT=g_words[e, o][:, j * P:(j + 1) * P].bitcast(E5M2),
                         lhsT_scale=g_planes[o][:, b * P:(b + 1) * P],
-                        rhs=w2_sb[:, g * 2 * H:(g + 1) * 2 * H].bitcast(E2M1),
+                        rhs=w2_sb[g // E][:, (g % E) * 2 * H:(g % E + 1) * 2 * H].bitcast(E2M1),
                         rhs_scale=w2_plane[:, g * H:(g + 1) * H],
                         start=(o == 0),
                         stop=(o == PASSES - 1),
                     )
-                dh_t = keep.tile([P, PACK, P], F32, name=f"dh_t{b}")
+                dh_t = keep.tile([P, PACK, P], F32, name="dh_t", bufs=2 * BLOCKS)
                 nc.scalar.activation(
                     out=dh_t[:], in_=acc[:].rearrange("p (m t) -> p t m", t=PACK), func=ACT.Copy,
                     scale=gate_col[:, b:b + 1],
@@ -162,37 +167,48 @@ def tile_moe_bdx_glu_relu_kernel(
 
         def masks_of(e):
             relu = a1_sb[e]
-            nc.scalar.activation(out=relu[:], in_=a1_sb[e][:], func=ACT.Relu)
             step = keep.tile([P, C, PACK], BF16, name=f"step{e}")
-            nc.scalar.activation(out=packed_by_pairs(step[:]), in_=by_pairs(relu[:]), func=ACT.Sign)
+            for cols in (slice(0, C // 2), slice(C // 2, C)):
+                nc.scalar.activation(out=relu[:, :, cols], in_=relu[:, :, cols], func=ACT.Relu)
+                nc.scalar.activation(out=packed_by_pairs(step[:, cols, :]), in_=by_pairs(relu[:, :, cols]), func=ACT.Sign)
             return relu, step
 
-        def quantise(da, name):
-            codes = ring.tile([P, C], U32, name=f"{name}_codes", align_bytes=64)
-            plane = ring.tile([P, C], U8, name=f"{name}_plane", align_bytes=64)
-            nc.vector.quantize_mx(out=codes[:].bitcast(E5M2), scales=plane[:], in_=da[:].rearrange("p c t -> p (c t)"))
-            return codes, plane
+        def quantise(codes, plane, da, cols):
+            nc.vector.quantize_mx(
+                out=codes[:, cols].bitcast(E5M2), scales=plane[:, cols], in_=da[:, cols, :].rearrange("p c t -> p (c t)"))
 
         def second_product(e, turned, relu, step):
             da1_full = ring.tile([P, C, PACK], BF16, name="da1_full", align_bytes=64)
             da1 = ring.tile([P, C, PACK], BF16, name="da1", align_bytes=64)
             da3 = ring.tile([P, C, PACK], BF16, name="da3", align_bytes=64)
+            codes1 = ring.tile([P, C], U32, name="codes1", align_bytes=64)
+            plane1 = ring.tile([P, C], U8, name="plane1", align_bytes=64)
+            codes3 = ring.tile([P, C], U32, name="codes3", align_bytes=64)
+            plane3 = ring.tile([P, C], U8, name="plane3", align_bytes=64)
+
+            def mask(engine, cols):
+                engine.tensor_tensor(out=da1[:, cols, :], in0=da1_full[:, cols, :], in1=step[:, cols, :], op=MULT)
+
             for j in range(BLOCKS):
                 cols = slice(j * P, (j + 1) * P)
                 dh = psum.tile([P, PACK, P], F32, name="dh", tag="d", bufs=4)
                 for t in range(PACK):
                     nc.tensor.transpose(dh[:, t, :], turned[j][:, t, :], ident[:])
-                nc.vector.tensor_tensor(
-                    out=packed_by_pairs(da1_full[:, cols, :]), in0=by_pairs(dh[:]), in1=by_pairs(a3_sb[e][:, :, cols]), op=MULT)
-                nc.vector.tensor_tensor(
-                    out=packed_by_pairs(da3[:, cols, :]), in0=by_pairs(dh[:]), in1=by_pairs(relu[:, :, cols]), op=MULT)
-            nc.vector.tensor_tensor(out=da1[:], in0=da1_full[:], in1=step[:], op=MULT)
-            q3 = quantise(da3, "da3")
-            q1 = quantise(da1, "da1")
+                products = [(da1_full, a3_sb[e]), (da3, relu)]
+                for da, saved in products if j < BLOCKS - 1 else reversed(products):
+                    nc.vector.tensor_tensor(
+                        out=packed_by_pairs(da[:, cols, :]), in0=by_pairs(dh[:]), in1=by_pairs(saved[:, :, cols]), op=MULT)
+                if j < BLOCKS - 1:
+                    mask(nc.gpsimd, cols)
+            quantise(codes3, plane3, da3, slice(0, C))
+            mask(nc.vector, slice(C - P, C))
+            quantise(codes1, plane1, da1, slice(0, C // 2))
+            quantise(codes1, plane1, da1, slice(C // 2, C))
+            passes = [(w3_sb, w3_plane, codes3, plane3), (w1_sb, w1_plane, codes1, plane1)]
             for kb in range(KB):
                 acc = psum.tile([P, C], F32, name="dx_ps", tag="x", bufs=2)
-                for i, (w_sb, w_plane, (codes, plane)) in enumerate(((w3_sb, w3_plane, q3), (w1_sb, w1_plane, q1))):
-                    c0 = e * K + kb * P
+                c0 = e * K + kb * P
+                for i, (w_sb, w_plane, codes, plane) in enumerate(passes if kb == 0 else reversed(passes)):
                     nc.tensor.matmul_mx(
                         out=acc[:],
                         lhsT=w_sb[:, 2 * c0:2 * (c0 + P)].bitcast(E2M1),
@@ -205,11 +221,12 @@ def tile_moe_bdx_glu_relu_kernel(
                 nc.scalar.copy(out=dx[kb][:, e * C:(e + 1) * C], in_=acc[:])
 
         ready = []
-        for e in range(E):
-            turned = first_product(e)
-            ready.append((turned,) + masks_of(e))
-        for e in range(E):
-            second_product(e, *ready[e])
+        for e in range(E + 1):
+            if e < E:
+                turned = first_product(e)
+                ready.append((turned,) + masks_of(e))
+            if e > 0:
+                second_product(e - 1, *ready[e - 1])
 
         firsts = []
         for kb in range(KB):

@@ -26,6 +26,7 @@ BLOCKS = C // P
 KB = K // P
 LIST_COLS = C // 16
 SHIFT = 16
+GPSIMD_SLOTS = 320
 
 
 def tile_moe_bdx_glu_relu_kernel(
@@ -157,7 +158,7 @@ def tile_moe_bdx_glu_relu_kernel(
                         start=(o == 0),
                         stop=(o == PASSES - 1),
                     )
-                dh_t = keep.tile([P, PACK, P], F32, name="dh_t", bufs=2 * BLOCKS)
+                dh_t = keep.tile([P, PACK, P], F32, name=f"dh_t{b}")
                 nc.scalar.activation(
                     out=dh_t[:], in_=acc[:].rearrange("p (m t) -> p t m", t=PACK), func=ACT.Copy,
                     scale=gate_col[:, b:b + 1],
@@ -189,24 +190,34 @@ def tile_moe_bdx_glu_relu_kernel(
             def mask(engine, cols):
                 engine.tensor_tensor(out=da1[:, cols, :], in0=da1_full[:, cols, :], in1=step[:, cols, :], op=MULT)
 
+            dh = []
             for j in range(BLOCKS):
-                cols = slice(j * P, (j + 1) * P)
-                dh = psum.tile([P, PACK, P], F32, name="dh", tag="d", bufs=4)
+                bank = psum.tile([P, PACK, P], F32, name="dh", tag="d", bufs=BLOCKS)
                 for t in range(PACK):
-                    nc.tensor.transpose(dh[:, t, :], turned[j][:, t, :], ident[:])
-                products = [(da1_full, a3_sb[e]), (da3, relu)]
-                for da, saved in products if j < BLOCKS - 1 else reversed(products):
-                    nc.vector.tensor_tensor(
-                        out=packed_by_pairs(da[:, cols, :]), in0=by_pairs(dh[:]), in1=by_pairs(saved[:, :, cols]), op=MULT)
-                if j < BLOCKS - 1:
-                    mask(nc.gpsimd, cols)
+                    nc.tensor.transpose(bank[:, t, :], turned[j][:, t, :], ident[:])
+                dh.append(bank)
+
+            def product(da, saved, j):
+                cols = slice(j * P, (j + 1) * P)
+                nc.vector.tensor_tensor(
+                    out=packed_by_pairs(da[:, cols, :]), in0=by_pairs(dh[j][:]), in1=by_pairs(saved[:, :, cols]), op=MULT)
+
+            product(da1_full, a3_sb[e], 0)
+            mask(nc.gpsimd, slice(0, P))
+            for j in range(1, BLOCKS - 1):
+                product(da1_full, a3_sb[e], j)
+            mask(nc.gpsimd, slice(P, GPSIMD_SLOTS))
+            for j in range(BLOCKS):
+                product(da3, relu, j)
+            product(da1_full, a3_sb[e], BLOCKS - 1)
             quantise(codes3, plane3, da3, slice(0, C))
-            mask(nc.vector, slice(C - P, C))
+            mask(nc.vector, slice(GPSIMD_SLOTS, C))
             quantise(codes1, plane1, da1, slice(0, C // 2))
             quantise(codes1, plane1, da1, slice(C // 2, C))
             passes = [(w3_sb, w3_plane, codes3, plane3), (w1_sb, w1_plane, codes1, plane1)]
+            sums = []
             for kb in range(KB):
-                acc = psum.tile([P, C], F32, name="dx_ps", tag="x", bufs=2)
+                acc = psum.tile([P, C], F32, name="dx_ps", tag="xh"[e % 2], bufs=2)
                 c0 = e * K + kb * P
                 for i, (w_sb, w_plane, codes, plane) in enumerate(passes if kb == 0 else reversed(passes)):
                     nc.tensor.matmul_mx(
@@ -218,15 +229,20 @@ def tile_moe_bdx_glu_relu_kernel(
                         start=(i == 0),
                         stop=(i == 1),
                     )
-                nc.scalar.copy(out=dx[kb][:, e * C:(e + 1) * C], in_=acc[:])
+                sums.append(acc)
+            return sums
 
-        ready = []
-        for e in range(E + 1):
-            if e < E:
-                turned = first_product(e)
-                ready.append((turned,) + masks_of(e))
-            if e > 0:
-                second_product(e - 1, *ready[e - 1])
+        def drain(e, sums):
+            for kb in range(KB):
+                nc.scalar.copy(out=dx[kb][:, e * C:(e + 1) * C], in_=sums[kb][:])
+
+        ready = [(first_product(e),) + masks_of(e) for e in range(2)]
+        sums = second_product(0, *ready[0])
+        ready.extend((first_product(e),) + masks_of(e) for e in range(2, E))
+        for e in range(1, E):
+            drain(e - 1, sums)
+            sums = second_product(e, *ready[e])
+        drain(E - 1, sums)
 
         firsts = []
         for kb in range(KB):

from contextlib import ExitStack

import concourse.mybir as mybir
from concourse.masks import make_identity

K, T, E, C, H, N = 256, 1024, 4, 512, 512, 1024
S = E * C
FLOPS = 2 * S * (N * H + 2 * H * K)

F32 = mybir.dt.float32
BF16 = mybir.dt.bfloat16
I32 = mybir.dt.int32
U32 = mybir.dt.uint32
U16 = mybir.dt.uint16
U8 = mybir.dt.uint8
E5M2 = mybir.dt.float8_e5m2_x4
E2M1 = mybir.dt.float4_e2m1fn_x4
ACT = mybir.ActivationFunctionType
MULT = mybir.AluOpType.mult
ADD = mybir.AluOpType.add

P = 128
PACK = 4
PASSES = N // (P * PACK)
BLOCKS = C // P
KB = K // P
LIST_COLS = C // 16
SHIFT = 16
GPSIMD_SLOTS = 320


def tile_moe_bdx_glu_relu_kernel(
    tc, dy_words, dy_scales, a1, a3, w2_words, w2_scales, w1_words, w1_scales, w3_words, w3_scales,
    gate, offs, pos1, pos2, out,
):
    nc = tc.nc
    with ExitStack() as ctx:
        lists = ctx.enter_context(tc.tile_pool(name="lists", bufs=1))
        keep = ctx.enter_context(tc.tile_pool(name="keep", bufs=1))
        ring = ctx.enter_context(tc.tile_pool(name="ring", bufs=2))
        psum = ctx.enter_context(tc.psum_pool(name="psum", bufs=1))

        offs_sb = lists.tile([P, S // 16], U16, name="offs_sb")
        pos1_sb = lists.tile([P, T // 16], U16, name="pos1_sb")
        pos2_sb = lists.tile([P, T // 16], U16, name="pos2_sb")

        dy_plane = keep.tile([P, T], U8, name="dy_plane", align_bytes=64)
        w2_plane = keep.tile([P, E * PASSES * H], U8, name="w2_plane", align_bytes=64)
        w1_plane = keep.tile([P, E * K], U8, name="w1_plane", align_bytes=64)
        w3_plane = keep.tile([P, E * K], U8, name="w3_plane", align_bytes=64)
        g_plane0 = keep.tile([P, S], U8, name="g_plane0", align_bytes=64)
        g_plane1 = keep.tile([P, S], U8, name="g_plane1", align_bytes=64)
        nc.gpsimd.memset(dy_plane[:].bitcast(I32), 0)
        for plane in (w2_plane, g_plane1, w1_plane, w3_plane):
            nc.vector.memset(plane[:].bitcast(I32), 0)
        gate_rows = keep.tile([P, P], F32, name="gate_rows")
        nc.gpsimd.memset(gate_rows[:], 0.0)
        ident = keep.tile([P, P], F32, name="ident")
        make_identity(nc, ident[:])

        def load_act(src, name, e, parts=1):
            t = keep.tile([P, PACK, C], F32, name=f"{name}{e}")
            for c0 in range(0, C, C // parts):
                c1 = c0 + C // parts
                nc.sync.dma_start(out=t[:, :, c0:c1], in_=src[:, e * C + c0:e * C + c1].rearrange("(p t) c -> p t c", t=PACK))
            return t

        def load_plane(plane, scales, width):
            for r in range(4):
                nc.sync.dma_start(
                    out=plane[r:P:32, :].bitcast(I32).rearrange("q (g c) -> q g c", c=width // 4),
                    in_=scales[:, :, r:16:4, :].rearrange("e s q c -> q (e s) c").bitcast(I32),
                )

        def load_words(words, name):
            groups, width = words.shape[0] * words.shape[1], words.shape[3]
            t = keep.tile([P, groups * width], U8, name=name, align_bytes=64)
            nc.sync.dma_start(
                out=t[:].bitcast(I32).rearrange("p (g c) -> p g c", g=groups),
                in_=words.rearrange("e s p c -> p (e s) c").bitcast(I32),
            )
            return t

        nc.sync.dma_start(offs_sb[:], offs)
        for r in range(4):
            nc.sync.dma_start(
                out=dy_plane[r:P:SHIFT, :].bitcast(I32),
                in_=dy_scales[:, r:16:4, :].rearrange("o q c -> q o c").bitcast(I32),
            )
        def load_dy(o):
            t = keep.tile([P, T], U32, name=f"dy{o}", align_bytes=64)
            nc.sync.dma_start(out=t[:].bitcast(I32), in_=dy_words[o].rearrange("p t d -> p (t d)").bitcast(I32))
            return t

        a1_sb, a3_sb = [None] * E, [None] * E
        a1_sb[0] = load_act(a1, "a1_", 0, parts=2)
        dy_sb = [load_dy(0)]
        a1_sb[1] = load_act(a1, "a1_", 1)
        dy_sb.append(load_dy(1))
        nc.sync.dma_start(out=gate_rows[0:S // P, :], in_=gate[0:1, :].rearrange("o (b c) -> (o b) c", c=P))
        load_plane(w2_plane, w2_scales, H)
        w2_sb = [load_words(w2_words[0:E // 2], "w2_lo")]

        def slots_of(e):
            return offs_sb[:, e * LIST_COLS:(e + 1) * LIST_COLS]

        for e in range(E):
            nc.vector.tensor_copy(out=g_plane0[:, e * C:(e + 1) * C], in_=dy_plane[:].indirect(slots_of(e)))
        nc.sync.dma_start(out=g_plane1[0:P - SHIFT, :].bitcast(I32), in_=g_plane0[SHIFT:P, :].bitcast(I32))
        w2_sb.append(load_words(w2_words[E // 2:E], "w2_hi"))
        a3_sb[0] = load_act(a3, "a3_", 0)
        a1_sb[2] = load_act(a1, "a1_", 2)
        load_plane(w1_plane, w1_scales, K)
        load_plane(w3_plane, w3_scales, K)
        w1_sb = load_words(w1_words, "w1_sb")
        w3_sb = load_words(w3_words, "w3_sb")
        a3_sb[1] = load_act(a3, "a3_", 1)
        a1_sb[3] = load_act(a1, "a1_", 3)
        a3_sb[2] = load_act(a3, "a3_", 2)
        a3_sb[3] = load_act(a3, "a3_", 3)
        nc.sync.dma_start(pos1_sb[:], pos1)
        nc.sync.dma_start(pos2_sb[:], pos2)

        gate_ps = psum.tile([P, C], F32, name="gate_ps", tag="x", bufs=2)
        nc.tensor.transpose(gate_ps[:, 0:P], gate_rows[:], ident[:])
        gate_col = keep.tile([P, S // P], F32, name="gate_col")
        nc.scalar.copy(out=gate_col[:], in_=gate_ps[:, 0:S // P])

        g_planes = (g_plane0, g_plane1)
        g_words = {}
        for e in range(E):
            for o in range(PASSES):
                t = keep.tile([P, C], U32, name=f"g{e}_{o}", align_bytes=64)
                nc.vector.tensor_copy(out=t[:], in_=dy_sb[o][:].indirect(slots_of(e)))
                g_words[e, o] = t

        dx = [keep.tile([P, S], F32, name=f"dx{kb}") for kb in range(KB)]

        def by_pairs(rows):
            return rows.rearrange("p t (c i) -> p c t i", i=2)

        def packed_by_pairs(cols):
            return cols.rearrange("p (c i) t -> p c t i", i=2)

        def first_product(e):
            turned = []
            for j in range(BLOCKS):
                b = e * BLOCKS + j
                acc = psum.tile([P, H], F32, name="acc", tag="h", bufs=2)
                for o in range(PASSES):
                    g = e * PASSES + o
                    nc.tensor.matmul_mx(
                        out=acc[:],
                        lhsT=g_words[e, o][:, j * P:(j + 1) * P].bitcast(E5M2),
                        lhsT_scale=g_planes[o][:, b * P:(b + 1) * P],
                        rhs=w2_sb[g // E][:, (g % E) * 2 * H:(g % E + 1) * 2 * H].bitcast(E2M1),
                        rhs_scale=w2_plane[:, g * H:(g + 1) * H],
                        start=(o == 0),
                        stop=(o == PASSES - 1),
                    )
                dh_t = keep.tile([P, PACK, P], F32, name=f"dh_t{b}")
                nc.scalar.activation(
                    out=dh_t[:], in_=acc[:].rearrange("p (m t) -> p t m", t=PACK), func=ACT.Copy,
                    scale=gate_col[:, b:b + 1],
                )
                turned.append(dh_t)
            return turned

        def masks_of(e):
            relu = a1_sb[e]
            step = keep.tile([P, C, PACK], BF16, name=f"step{e}")
            for cols in (slice(0, C // 2), slice(C // 2, C)):
                nc.scalar.activation(out=relu[:, :, cols], in_=relu[:, :, cols], func=ACT.Relu)
                nc.scalar.activation(out=packed_by_pairs(step[:, cols, :]), in_=by_pairs(relu[:, :, cols]), func=ACT.Sign)
            return relu, step

        def quantise(codes, plane, da, cols):
            nc.vector.quantize_mx(
                out=codes[:, cols].bitcast(E5M2), scales=plane[:, cols], in_=da[:, cols, :].rearrange("p c t -> p (c t)"))

        def second_product(e, turned, relu, step):
            da1_full = ring.tile([P, C, PACK], BF16, name="da1_full", align_bytes=64)
            da1 = ring.tile([P, C, PACK], BF16, name="da1", align_bytes=64)
            da3 = ring.tile([P, C, PACK], BF16, name="da3", align_bytes=64)
            codes1 = ring.tile([P, C], U32, name="codes1", align_bytes=64)
            plane1 = ring.tile([P, C], U8, name="plane1", align_bytes=64)
            codes3 = ring.tile([P, C], U32, name="codes3", align_bytes=64)
            plane3 = ring.tile([P, C], U8, name="plane3", align_bytes=64)

            def mask(engine, cols):
                engine.tensor_tensor(out=da1[:, cols, :], in0=da1_full[:, cols, :], in1=step[:, cols, :], op=MULT)

            dh = []
            for j in range(BLOCKS):
                bank = psum.tile([P, PACK, P], F32, name="dh", tag="d", bufs=BLOCKS)
                for t in range(PACK):
                    nc.tensor.transpose(bank[:, t, :], turned[j][:, t, :], ident[:])
                dh.append(bank)

            def product(da, saved, j):
                cols = slice(j * P, (j + 1) * P)
                nc.vector.tensor_tensor(
                    out=packed_by_pairs(da[:, cols, :]), in0=by_pairs(dh[j][:]), in1=by_pairs(saved[:, :, cols]), op=MULT)

            product(da1_full, a3_sb[e], 0)
            mask(nc.gpsimd, slice(0, P))
            for j in range(1, BLOCKS - 1):
                product(da1_full, a3_sb[e], j)
            mask(nc.gpsimd, slice(P, GPSIMD_SLOTS))
            for j in range(BLOCKS):
                product(da3, relu, j)
            product(da1_full, a3_sb[e], BLOCKS - 1)
            quantise(codes3, plane3, da3, slice(0, C))
            mask(nc.vector, slice(GPSIMD_SLOTS, C))
            quantise(codes1, plane1, da1, slice(0, C // 2))
            quantise(codes1, plane1, da1, slice(C // 2, C))
            passes = [(w3_sb, w3_plane, codes3, plane3), (w1_sb, w1_plane, codes1, plane1)]
            sums = []
            for kb in range(KB):
                acc = psum.tile([P, C], F32, name="dx_ps", tag="xh"[e % 2], bufs=2)
                c0 = e * K + kb * P
                for i, (w_sb, w_plane, codes, plane) in enumerate(passes if kb == 0 else reversed(passes)):
                    nc.tensor.matmul_mx(
                        out=acc[:],
                        lhsT=w_sb[:, 2 * c0:2 * (c0 + P)].bitcast(E2M1),
                        lhsT_scale=w_plane[:, c0:c0 + P],
                        rhs=codes[:].bitcast(E5M2),
                        rhs_scale=plane[:],
                        start=(i == 0),
                        stop=(i == 1),
                    )
                sums.append(acc)
            return sums

        def drain(e, sums):
            for kb in range(KB):
                nc.scalar.copy(out=dx[kb][:, e * C:(e + 1) * C], in_=sums[kb][:])

        ready = [(first_product(e),) + masks_of(e) for e in range(2)]
        sums = second_product(0, *ready[0])
        ready.extend((first_product(e),) + masks_of(e) for e in range(2, E))
        for e in range(1, E):
            drain(e - 1, sums)
            sums = second_product(e, *ready[e])
        drain(E - 1, sums)

        firsts = []
        for kb in range(KB):
            first = keep.tile([P, T], F32, name=f"first{kb}")
            nc.vector.tensor_copy(out=first[:], in_=dx[kb][:].indirect(pos1_sb[:]))
            firsts.append(first)
        pieces = [(0, 0, T), (1, 0, T // 2), (1, T // 2, T // 4), (1, 3 * T // 4, T // 4)]
        for kb, t0, n in pieces:
            both = keep.tile([P, n], F32, name=f"both{kb}_{t0}")
            nc.vector.tensor_tensor(
                out=both[:], in0=dx[kb][:].indirect(pos2_sb[:, t0 // 16:(t0 + n) // 16]), in1=firsts[kb][:, t0:t0 + n], op=ADD)
            nc.sync.dma_start(out=out[kb * P:(kb + 1) * P, t0:t0 + n], in_=both[:])
